import numpy as np
import ml_dtypes


def mxq(x, axis, fmt="e4m3"):
    dtype, down = {"e4m3": (ml_dtypes.float8_e4m3fn, 7), "e5m2": (ml_dtypes.float8_e5m2, 14)}[fmt]
    v = np.moveaxis(np.asarray(x, np.float32).astype(ml_dtypes.bfloat16).astype(np.float64), axis, -1)
    blocks = v.reshape(v.shape[:-1] + (-1, 32))
    amax = np.abs(blocks).max(-1, keepdims=True)
    byte = np.maximum(np.where(amax > 0, np.frexp(amax)[1] - 1 + 127, 0) - down, 1)
    scale = np.exp2(byte - 127.0)
    codes = (blocks / scale).astype(np.float32).astype(dtype).astype(np.float64)
    return np.moveaxis((codes * scale).reshape(v.shape), -1, axis)


WIDE = False


def mx_kscale(k):
    if not WIDE:
        return np.ones(k)
    levels = np.array([10, -10, 5, -5, 0])
    if k % 512:
        return np.exp2(np.random.permutation(np.resize(levels, k // 32))).repeat(32)
    a = np.empty((k // 512, 16))
    for p in range(k // 512):
        a[p, :8] = np.random.permutation(np.resize(levels, 8))
        for g in range(8):
            far = levels[np.abs(levels - a[p, g]) >= 10]
            a[p, g + 8] = far[np.random.randint(len(far))]
    return np.exp2(a.ravel()).repeat(32)


def f64(x):
    return np.asarray(x).astype(np.float64)


def striped(idx):
    return np.tile(np.asarray(idx).reshape(-1, 16).T, (8, 1)).astype(np.uint16)


def unstriped(offs):
    return offs[:16].T.reshape(-1).astype(np.int64)


E2M1 = np.array([0.0, 0.5, 1.0, 1.5, 2.0, 3.0, 4.0, 6.0, -0.0, -0.5, -1.0, -1.5, -2.0, -3.0, -4.0, -6.0])


def pack_weight(w, fmt):
    k, n = w.shape
    w = f64(np.asarray(w, np.float32).astype(ml_dtypes.bfloat16)).reshape(k // 32, 32, n)
    amax = np.abs(w).max(1)
    if fmt == "e4m3":
        byte = np.frexp(amax)[1] - 1 + 127 - 7
    else:
        mant, ex = np.frexp(amax / 6.0)
        byte = np.where(mant > 0.5, ex, ex - 1) + 127
    byte = np.clip(np.where(amax > 0, byte, 1), 1, 254)
    scaled = (w * np.exp2(127.0 - byte)[:, None, :]).reshape(k, n).astype(np.float32)
    by_word = np.ascontiguousarray(scaled.reshape(k // 512, 128, 4, n).transpose(0, 1, 3, 2))
    if fmt == "e4m3":
        words = by_word.astype(ml_dtypes.float8_e4m3fn).view(np.uint8)
    else:
        c = by_word.astype(ml_dtypes.float4_e2m1fn).view(np.uint8) & 0xF
        words = (c[..., 0::2] | (c[..., 1::2] << 4)).reshape(k // 512, 128, 2 * n)
    return np.ascontiguousarray(words), np.ascontiguousarray(byte.astype(np.uint8).reshape(k // 512, 16, n))


def unpack_weight(words, scales, fmt):
    g, _, n = scales.shape
    words = np.ascontiguousarray(words).reshape(g, 128, n, -1)
    if fmt == "e4m3":
        vals = words.view(ml_dtypes.float8_e4m3fn).astype(np.float64)
    else:
        nib = np.empty((g, 128, n, 4), np.uint8)
        nib[..., 0::2] = words & 0xF
        nib[..., 1::2] = words >> 4
        vals = E2M1[nib]
    vals = vals * np.repeat(np.exp2(scales.astype(np.float64) - 127.0), 8, axis=1)[..., None]
    return vals.transpose(0, 1, 3, 2).reshape(g * 512, n)


B, N, T, D, NQ = 1, 512, 2048, 512, 256


def setup_inputs():
    n = np.random.standard_normal
    idx = np.random.permutation(T)[:B * N]
    s = mx_kscale(D)[:, None]
    kp = pack_weight(n((D, T)) / s, "e4m3")
    return {
        "qT": (n((B, D, NQ)) * s * (1.00 / np.sqrt(D))).astype(np.float32),
        "k_words": kp[0],
        "k_scales": kp[1],
        "offs": striped(idx),
    }


def reference(qT, k_words, k_scales, offs):
    idx = unstriped(offs)
    pick = lambda x, which: x[:, which].reshape(x.shape[0], B, -1).transpose(1, 0, 2)
    k = unpack_weight(k_words, k_scales, "e4m3")
    kg = pick(k, idx)
    qq = mxq(f64(qT), 1, "e4m3")
    a = qq.transpose(0, 2, 1) @ kg
    y = a / np.sqrt(np.sum(np.square(a), axis=-1, keepdims=True) + 0.0001)
    return y

@@ -1,0 +1,112 @@
+from contextlib import ExitStack
+
+import concourse.mybir as mybir
+
+F32 = mybir.dt.float32
+BF16 = mybir.dt.bfloat16
+I32 = mybir.dt.int32
+U32 = mybir.dt.uint32
+U16 = mybir.dt.uint16
+U8 = mybir.dt.uint8
+FP8X4 = mybir.dt.float8_e4m3fn_x4
+ACT = mybir.ActivationFunctionType
+ALU = mybir.AluOpType
+
+P = 128
+PACK = 4
+D, NQ, T, N = 512, 256, 2048, 512
+HALF = N // 2
+FLOPS = 2 * NQ * N * D
+
+
+def tile_attend_nrm_topk_kernel(tc, qT, k_words, k_scales, offs, out):
+    nc = tc.nc
+    with ExitStack() as ctx:
+        sb = ctx.enter_context(tc.tile_pool(name="sb", bufs=1))
+        ps = ctx.enter_context(tc.psum_pool(name="ps", bufs=1))
+
+        offsets = sb.tile([P, N // 16], U16, name="offsets")
+        q_raw = sb.tile([P, PACK, NQ], F32, name="q_raw")
+        pool_scales = sb.tile([P, T], U8, name="pool_scales", align_bytes=64)
+        pool_words = sb.tile([P, T], U32, name="pool_words", align_bytes=64)
+        ones = sb.tile([P, 1], F32, name="ones")
+        eps = sb.tile([P, 1], F32, name="eps")
+
+        nc.vector.memset(pool_scales[:].bitcast(I32), 0)
+        nc.gpsimd.memset(ones[:], 1.0)
+        nc.scalar.activation(eps[:], ones[:], ACT.Abs_reciprocal_sqrt, scale=1e8)
+
+        nc.sync.dma_start(out=q_raw[:], in_=qT[0].rearrange("(p j) w -> p j w", j=PACK))
+        nc.sync.dma_start(offsets[:], offs)
+        scale_rows = k_scales[0].rearrange("(g r) t -> r g t", r=4)
+        for r in range(4):
+            nc.sync.dma_start(out=pool_scales[r:P:32, :].bitcast(I32), in_=scale_rows[r].bitcast(I32))
+        nc.sync.dma_start(
+            out=pool_words[:].bitcast(I32),
+            in_=k_words[0].rearrange("p t r -> p (t r)").bitcast(I32),
+        )
+
+        q_bf = [sb.tile([P, P, PACK], BF16, name="q_bf%d" % c, align_bytes=64) for c in range(2)]
+        q_codes = [sb.tile([P, P], U32, name="q_codes%d" % c, align_bytes=64) for c in range(2)]
+        q_scales = [sb.tile([P, P], U8, name="q_scales%d" % c, align_bytes=64) for c in range(2)]
+        nc.vector.tensor_copy(out=q_bf[0][:], in_=q_raw[:, :, 0:P].rearrange("p j w -> p w j"))
+        nc.scalar.copy(out=q_bf[1][:], in_=q_raw[:, :, P:NQ].rearrange("p j w -> p w j"))
+
+        key_scales = sb.tile([P, N], U8, name="key_scales", align_bytes=64)
+        nc.vector.tensor_copy(key_scales[:], pool_scales[:].indirect(offsets[:]))
+
+        for c in range(2):
+            nc.vector.quantize_mx(
+                out=q_codes[c][:].bitcast(FP8X4),
+                scales=q_scales[c][:],
+                in_=q_bf[c][:].rearrange("p w j -> p (w j)"),
+            )
+
+        key_words = [sb.tile([P, HALF], U32, name="key_words%d" % h, align_bytes=64) for h in range(2)]
+        for h in range(2):
+            nc.vector.tensor_copy(key_words[h][:], pool_words[:].indirect(offsets[:, 16 * h : 16 * (h + 1)]))
+
+        acc = [[ps.tile([P, HALF], F32, name="acc%d%d" % (c, h)) for h in range(2)] for c in range(2)]
+        squares = sb.tile([P, HALF], BF16, name="squares")
+        ss = [[sb.tile([P, 1], F32, name="ss%d%d" % (c, h)) for h in range(2)] for c in range(2)]
+        bias = [sb.tile([P, 1], F32, name="bias%d" % c) for c in range(2)]
+        rinv = [sb.tile([P, 1], F32, name="rinv%d" % c) for c in range(2)]
+        first = [sb.tile([P, HALF], F32, name="first%d" % c) for c in range(2)]
+        res = [[sb.tile([P, HALF], F32, name="res%d%d" % (c, h)) for h in range(2)] for c in range(2)]
+
+        def product(c, h):
+            nc.tensor.matmul_mx(
+                out=acc[c][h][:],
+                lhsT=q_codes[c][:].bitcast(FP8X4),
+                lhsT_scale=q_scales[c][:],
+                rhs=key_words[h][:].bitcast(FP8X4),
+                rhs_scale=key_scales[:, h * HALF : (h + 1) * HALF],
+                start=True,
+                stop=True,
+            )
+
+        def square(c, h):
+            nc.scalar.activation(squares[:], acc[c][h][:], ACT.Square, accum_out=ss[c][h][:])
+
+        def store(c, h, engine):
+            engine.dma_start(out=out[0, c * P : (c + 1) * P, h * HALF : (h + 1) * HALF], in_=res[c][h][:])
+
+        for h in range(2):
+            for c in range(2):
+                product(c, h)
+        for c in range(2):
+            square(c, 0)
+            nc.vector.tensor_scalar(bias[c][:], ss[c][0][:], eps[:], None, ALU.add)
+        for c in range(2):
+            nc.vector.tensor_copy(first[c][:], acc[c][0][:])
+        for c in range(2):
+            square(c, 1)
+            nc.scalar.activation(rinv[c][:], ss[c][1][:], ACT.Abs_reciprocal_sqrt, bias=bias[c][:])
+        nc.vector.tensor_scalar(res[0][0][:], first[0][:], rinv[0][:], None, ALU.mult)
+        store(0, 0, nc.sync)
+        nc.vector.tensor_scalar(res[0][1][:], acc[0][1][:], rinv[0][:], None, ALU.mult)
+        store(0, 1, nc.sync)
+        nc.vector.tensor_scalar(res[1][0][:], first[1][:], rinv[1][:], None, ALU.mult)
+        store(1, 0, nc.sync)
+        nc.scalar.activation(res[1][1][:], acc[1][1][:], ACT.Copy, scale=rinv[1][:])
+        store(1, 1, nc.scalar)

@@ -26,7 +26,7 @@ def tile_attend_nrm_topk_kernel(tc, qT, k_words, k_scales, offs, out):
         ps = ctx.enter_context(tc.psum_pool(name="ps", bufs=1))
 
         offsets = sb.tile([P, N // 16], U16, name="offsets")
-        q_raw = sb.tile([P, PACK, NQ], F32, name="q_raw")
+        q_raw = [sb.tile([P, PACK, P], F32, name="q_raw%d" % c) for c in range(2)]
         pool_scales = sb.tile([P, T], U8, name="pool_scales", align_bytes=64)
         pool_words = sb.tile([P, T], U32, name="pool_words", align_bytes=64)
         ones = sb.tile([P, 1], F32, name="ones")
@@ -36,42 +36,50 @@ def tile_attend_nrm_topk_kernel(tc, qT, k_words, k_scales, offs, out):
         nc.gpsimd.memset(ones[:], 1.0)
         nc.scalar.activation(eps[:], ones[:], ACT.Abs_reciprocal_sqrt, scale=1e8)
 
-        nc.sync.dma_start(out=q_raw[:], in_=qT[0].rearrange("(p j) w -> p j w", j=PACK))
+        q_rows = qT[0].rearrange("(p j) w -> p j w", j=PACK)
+        nc.sync.dma_start(out=q_raw[0][:], in_=q_rows[:, :, 0:P])
         nc.sync.dma_start(offsets[:], offs)
+        words = k_words[0].rearrange("p t r -> p (t r)").bitcast(I32)
+        nc.sync.dma_start(out=pool_words[:, 0:512].bitcast(I32), in_=words[:, 0:512])
         scale_rows = k_scales[0].rearrange("(g r) t -> r g t", r=4)
         for r in range(4):
             nc.sync.dma_start(out=pool_scales[r:P:32, :].bitcast(I32), in_=scale_rows[r].bitcast(I32))
-        nc.sync.dma_start(
-            out=pool_words[:].bitcast(I32),
-            in_=k_words[0].rearrange("p t r -> p (t r)").bitcast(I32),
-        )
+        nc.sync.dma_start(out=pool_words[:, 512:T].bitcast(I32), in_=words[:, 512:T])
+        nc.sync.dma_start(out=q_raw[1][:], in_=q_rows[:, :, P:NQ])
 
         q_bf = [sb.tile([P, P, PACK], BF16, name="q_bf%d" % c, align_bytes=64) for c in range(2)]
         q_codes = [sb.tile([P, P], U32, name="q_codes%d" % c, align_bytes=64) for c in range(2)]
         q_scales = [sb.tile([P, P], U8, name="q_scales%d" % c, align_bytes=64) for c in range(2)]
-        nc.vector.tensor_copy(out=q_bf[0][:], in_=q_raw[:, :, 0:P].rearrange("p j w -> p w j"))
-        nc.scalar.copy(out=q_bf[1][:], in_=q_raw[:, :, P:NQ].rearrange("p j w -> p w j"))
 
-        key_scales = sb.tile([P, N], U8, name="key_scales", align_bytes=64)
-        nc.vector.tensor_copy(key_scales[:], pool_scales[:].indirect(offsets[:]))
-
-        for c in range(2):
+        def quantize(c):
             nc.vector.quantize_mx(
                 out=q_codes[c][:].bitcast(FP8X4),
                 scales=q_scales[c][:],
                 in_=q_bf[c][:].rearrange("p w j -> p (w j)"),
             )
 
+        nc.vector.tensor_copy(out=q_bf[0][:], in_=q_raw[0][:].rearrange("p j w -> p w j"))
+        quantize(0)
+
+        key_scales = sb.tile([P, N], U8, name="key_scales", align_bytes=64)
+        nc.vector.tensor_copy(key_scales[:], pool_scales[:].indirect(offsets[:]))
+
         key_words = [sb.tile([P, HALF], U32, name="key_words%d" % h, align_bytes=64) for h in range(2)]
         for h in range(2):
             nc.vector.tensor_copy(key_words[h][:], pool_words[:].indirect(offsets[:, 16 * h : 16 * (h + 1)]))
 
+        nc.scalar.copy(
+            out=q_bf[1][:].rearrange("p (c i) j -> p c j i", i=4),
+            in_=q_raw[1][:].rearrange("p j (c i) -> p c j i", i=4),
+        )
+        quantize(1)
+
         acc = [[ps.tile([P, HALF], F32, name="acc%d%d" % (c, h)) for h in range(2)] for c in range(2)]
-        squares = sb.tile([P, HALF], BF16, name="squares")
+        squares = [sb.tile([P, HALF], BF16, name="squares%d" % i) for i in range(3)]
         ss = [[sb.tile([P, 1], F32, name="ss%d%d" % (c, h)) for h in range(2)] for c in range(2)]
         bias = [sb.tile([P, 1], F32, name="bias%d" % c) for c in range(2)]
         rinv = [sb.tile([P, 1], F32, name="rinv%d" % c) for c in range(2)]
-        first = [sb.tile([P, HALF], F32, name="first%d" % c) for c in range(2)]
+        first = sb.tile([P, HALF], F32, name="first")
         res = [[sb.tile([P, HALF], F32, name="res%d%d" % (c, h)) for h in range(2)] for c in range(2)]
 
         def product(c, h):
@@ -86,27 +94,30 @@ def tile_attend_nrm_topk_kernel(tc, qT, k_words, k_scales, offs, out):
             )
 
         def square(c, h):
-            nc.scalar.activation(squares[:], acc[c][h][:], ACT.Square, accum_out=ss[c][h][:])
+            nc.scalar.activation(squares[(0, 1, 1, 2)[2 * c + h]][:], acc[c][h][:], ACT.Square, accum_out=ss[c][h][:])
 
         def store(c, h, engine):
             engine.dma_start(out=out[0, c * P : (c + 1) * P, h * HALF : (h + 1) * HALF], in_=res[c][h][:])
 
-        for h in range(2):
-            for c in range(2):
-                product(c, h)
         for c in range(2):
+            for h in range(2):
+                product(c, h)
+
+        def norm(c):
             square(c, 0)
             nc.vector.tensor_scalar(bias[c][:], ss[c][0][:], eps[:], None, ALU.add)
-        for c in range(2):
-            nc.vector.tensor_copy(first[c][:], acc[c][0][:])
-        for c in range(2):
+            if c == 0:
+                nc.vector.tensor_copy(first[:], acc[0][0][:])
             square(c, 1)
             nc.scalar.activation(rinv[c][:], ss[c][1][:], ACT.Abs_reciprocal_sqrt, bias=bias[c][:])
-        nc.vector.tensor_scalar(res[0][0][:], first[0][:], rinv[0][:], None, ALU.mult)
+
+        norm(0)
+        nc.vector.tensor_scalar(res[0][0][:], first[:], rinv[0][:], None, ALU.mult)
         store(0, 0, nc.sync)
+        norm(1)
         nc.vector.tensor_scalar(res[0][1][:], acc[0][1][:], rinv[0][:], None, ALU.mult)
         store(0, 1, nc.sync)
-        nc.vector.tensor_scalar(res[1][0][:], first[1][:], rinv[1][:], None, ALU.mult)
+        nc.vector.tensor_scalar(res[1][0][:], acc[1][0][:], rinv[1][:], None, ALU.mult)
         store(1, 0, nc.sync)
         nc.scalar.activation(res[1][1][:], acc[1][1][:], ACT.Copy, scale=rinv[1][:])
         store(1, 1, nc.scalar)

@@ -16,6 +16,7 @@ P = 128
 PACK = 4
 D, NQ, T, N = 512, 256, 2048, 512
 HALF = N // 2
+LEAD = 768
 FLOPS = 2 * NQ * N * D
 
 
@@ -36,16 +37,16 @@ def tile_attend_nrm_topk_kernel(tc, qT, k_words, k_scales, offs, out):
         nc.gpsimd.memset(ones[:], 1.0)
         nc.scalar.activation(eps[:], ones[:], ACT.Abs_reciprocal_sqrt, scale=1e8)
 
-        q_rows = qT[0].rearrange("(p j) w -> p j w", j=PACK)
-        nc.sync.dma_start(out=q_raw[0][:], in_=q_rows[:, :, 0:P])
-        nc.sync.dma_start(offsets[:], offs)
         words = k_words[0].rearrange("p t r -> p (t r)").bitcast(I32)
-        nc.sync.dma_start(out=pool_words[:, 0:512].bitcast(I32), in_=words[:, 0:512])
+        nc.sync.dma_start(out=pool_words[:, 0:LEAD].bitcast(I32), in_=words[:, 0:LEAD])
+        nc.sync.dma_start(offsets[:], offs)
         scale_rows = k_scales[0].rearrange("(g r) t -> r g t", r=4)
         for r in range(4):
             nc.sync.dma_start(out=pool_scales[r:P:32, :].bitcast(I32), in_=scale_rows[r].bitcast(I32))
-        nc.sync.dma_start(out=pool_words[:, 512:T].bitcast(I32), in_=words[:, 512:T])
-        nc.sync.dma_start(out=q_raw[1][:], in_=q_rows[:, :, P:NQ])
+        nc.sync.dma_start(out=pool_words[:, LEAD:T].bitcast(I32), in_=words[:, LEAD:T])
+        q_rows = qT[0].rearrange("(p j) w -> p j w", j=PACK)
+        for c in range(2):
+            nc.sync.dma_start(out=q_raw[c][:], in_=q_rows[:, :, c * P : (c + 1) * P])
 
         q_bf = [sb.tile([P, P, PACK], BF16, name="q_bf%d" % c, align_bytes=64) for c in range(2)]
         q_codes = [sb.tile([P, P], U32, name="q_codes%d" % c, align_bytes=64) for c in range(2)]
@@ -58,8 +59,6 @@ def tile_attend_nrm_topk_kernel(tc, qT, k_words, k_scales, offs, out):
                 in_=q_bf[c][:].rearrange("p w j -> p (w j)"),
             )
 
-        nc.vector.tensor_copy(out=q_bf[0][:], in_=q_raw[0][:].rearrange("p j w -> p w j"))
-        quantize(0)
 
         key_scales = sb.tile([P, N], U8, name="key_scales", align_bytes=64)
         nc.vector.tensor_copy(key_scales[:], pool_scales[:].indirect(offsets[:]))
@@ -68,18 +67,19 @@ def tile_attend_nrm_topk_kernel(tc, qT, k_words, k_scales, offs, out):
         for h in range(2):
             nc.vector.tensor_copy(key_words[h][:], pool_words[:].indirect(offsets[:, 16 * h : 16 * (h + 1)]))
 
-        nc.scalar.copy(
-            out=q_bf[1][:].rearrange("p (c i) j -> p c j i", i=4),
-            in_=q_raw[1][:].rearrange("p j (c i) -> p c j i", i=4),
-        )
-        quantize(1)
+        for c in range(2):
+            nc.scalar.copy(
+                out=q_bf[c][:].rearrange("p (g i) j -> p g j i", i=4),
+                in_=q_raw[c][:].rearrange("p j (g i) -> p g j i", i=4),
+            )
+            quantize(c)
 
         acc = [[ps.tile([P, HALF], F32, name="acc%d%d" % (c, h)) for h in range(2)] for c in range(2)]
-        squares = [sb.tile([P, HALF], BF16, name="squares%d" % i) for i in range(3)]
+        squares = [sb.tile([P, HALF], BF16, name="squares%d" % i) for i in range(4)]
         ss = [[sb.tile([P, 1], F32, name="ss%d%d" % (c, h)) for h in range(2)] for c in range(2)]
         bias = [sb.tile([P, 1], F32, name="bias%d" % c) for c in range(2)]
         rinv = [sb.tile([P, 1], F32, name="rinv%d" % c) for c in range(2)]
-        first = sb.tile([P, HALF], F32, name="first")
+        held = [sb.tile([P, HALF], F32, name="held%d" % i) for i in range(3)]
         res = [[sb.tile([P, HALF], F32, name="res%d%d" % (c, h)) for h in range(2)] for c in range(2)]
 
         def product(c, h):
@@ -94,7 +94,7 @@ def tile_attend_nrm_topk_kernel(tc, qT, k_words, k_scales, offs, out):
             )
 
         def square(c, h):
-            nc.scalar.activation(squares[(0, 1, 1, 2)[2 * c + h]][:], acc[c][h][:], ACT.Square, accum_out=ss[c][h][:])
+            nc.scalar.activation(squares[2 * c + h][:], acc[c][h][:], ACT.Square, accum_out=ss[c][h][:])
 
         def store(c, h, engine):
             engine.dma_start(out=out[0, c * P : (c + 1) * P, h * HALF : (h + 1) * HALF], in_=res[c][h][:])
@@ -103,21 +103,22 @@ def tile_attend_nrm_topk_kernel(tc, qT, k_words, k_scales, offs, out):
             for h in range(2):
                 product(c, h)
 
-        def norm(c):
-            square(c, 0)
-            nc.vector.tensor_scalar(bias[c][:], ss[c][0][:], eps[:], None, ALU.add)
-            if c == 0:
-                nc.vector.tensor_copy(first[:], acc[0][0][:])
-            square(c, 1)
-            nc.scalar.activation(rinv[c][:], ss[c][1][:], ACT.Abs_reciprocal_sqrt, bias=bias[c][:])
-
-        norm(0)
-        nc.vector.tensor_scalar(res[0][0][:], first[:], rinv[0][:], None, ALU.mult)
+        square(0, 0)
+        nc.vector.tensor_scalar(bias[0][:], ss[0][0][:], eps[:], None, ALU.add)
+        nc.vector.tensor_copy(held[0][:], acc[0][0][:])
+        square(0, 1)
+        nc.vector.tensor_copy(held[1][:], acc[0][1][:])
+        nc.scalar.activation(rinv[0][:], ss[0][1][:], ACT.Abs_reciprocal_sqrt, bias=bias[0][:])
+        square(1, 0)
+        nc.vector.tensor_scalar(bias[1][:], ss[1][0][:], eps[:], None, ALU.add)
+        nc.vector.tensor_copy(held[2][:], acc[1][0][:])
+        square(1, 1)
+        nc.scalar.activation(rinv[1][:], ss[1][1][:], ACT.Abs_reciprocal_sqrt, bias=bias[1][:])
+        nc.vector.tensor_scalar(res[0][0][:], held[0][:], rinv[0][:], None, ALU.mult)
         store(0, 0, nc.sync)
-        norm(1)
-        nc.vector.tensor_scalar(res[0][1][:], acc[0][1][:], rinv[0][:], None, ALU.mult)
+        nc.vector.tensor_scalar(res[0][1][:], held[1][:], rinv[0][:], None, ALU.mult)
         store(0, 1, nc.sync)
-        nc.vector.tensor_scalar(res[1][0][:], acc[1][0][:], rinv[1][:], None, ALU.mult)
+        nc.vector.tensor_scalar(res[1][0][:], held[2][:], rinv[1][:], None, ALU.mult)
         store(1, 0, nc.sync)
         nc.scalar.activation(res[1][1][:], acc[1][1][:], ACT.Copy, scale=rinv[1][:])
         store(1, 1, nc.scalar)

@@ -16,7 +16,7 @@ P = 128
 PACK = 4
 D, NQ, T, N = 512, 256, 2048, 512
 HALF = N // 2
-LEAD = 768
+LEAD = 896
 FLOPS = 2 * NQ * N * D
 
 
@@ -34,7 +34,7 @@ def tile_attend_nrm_topk_kernel(tc, qT, k_words, k_scales, offs, out):
         eps = sb.tile([P, 1], F32, name="eps")
 
         nc.vector.memset(pool_scales[:].bitcast(I32), 0)
-        nc.gpsimd.memset(ones[:], 1.0)
+        nc.vector.memset(ones[:], 1.0)
         nc.scalar.activation(eps[:], ones[:], ACT.Abs_reciprocal_sqrt, scale=1e8)
 
         words = k_words[0].rearrange("p t r -> p (t r)").bitcast(I32)
@@ -52,27 +52,21 @@ def tile_attend_nrm_topk_kernel(tc, qT, k_words, k_scales, offs, out):
         q_codes = [sb.tile([P, P], U32, name="q_codes%d" % c, align_bytes=64) for c in range(2)]
         q_scales = [sb.tile([P, P], U8, name="q_scales%d" % c, align_bytes=64) for c in range(2)]
 
-        def quantize(c):
-            nc.vector.quantize_mx(
-                out=q_codes[c][:].bitcast(FP8X4),
-                scales=q_scales[c][:],
-                in_=q_bf[c][:].rearrange("p w j -> p (w j)"),
-            )
-
-
         key_scales = sb.tile([P, N], U8, name="key_scales", align_bytes=64)
         nc.vector.tensor_copy(key_scales[:], pool_scales[:].indirect(offsets[:]))
-
-        key_words = [sb.tile([P, HALF], U32, name="key_words%d" % h, align_bytes=64) for h in range(2)]
-        for h in range(2):
-            nc.vector.tensor_copy(key_words[h][:], pool_words[:].indirect(offsets[:, 16 * h : 16 * (h + 1)]))
+        key_words = sb.tile([P, N], U32, name="key_words", align_bytes=64)
+        nc.vector.tensor_copy(key_words[:], pool_words[:].indirect(offsets[:]))
 
         for c in range(2):
             nc.scalar.copy(
                 out=q_bf[c][:].rearrange("p (g i) j -> p g j i", i=4),
                 in_=q_raw[c][:].rearrange("p j (g i) -> p g j i", i=4),
             )
-            quantize(c)
+            nc.vector.quantize_mx(
+                out=q_codes[c][:].bitcast(FP8X4),
+                scales=q_scales[c][:],
+                in_=q_bf[c][:].rearrange("p w j -> p (w j)"),
+            )
 
         acc = [[ps.tile([P, HALF], F32, name="acc%d%d" % (c, h)) for h in range(2)] for c in range(2)]
         squares = [sb.tile([P, HALF], BF16, name="squares%d" % i) for i in range(4)]
@@ -82,17 +76,6 @@ def tile_attend_nrm_topk_kernel(tc, qT, k_words, k_scales, offs, out):
         held = [sb.tile([P, HALF], F32, name="held%d" % i) for i in range(3)]
         res = [[sb.tile([P, HALF], F32, name="res%d%d" % (c, h)) for h in range(2)] for c in range(2)]
 
-        def product(c, h):
-            nc.tensor.matmul_mx(
-                out=acc[c][h][:],
-                lhsT=q_codes[c][:].bitcast(FP8X4),
-                lhsT_scale=q_scales[c][:],
-                rhs=key_words[h][:].bitcast(FP8X4),
-                rhs_scale=key_scales[:, h * HALF : (h + 1) * HALF],
-                start=True,
-                stop=True,
-            )
-
         def square(c, h):
             nc.scalar.activation(squares[2 * c + h][:], acc[c][h][:], ACT.Square, accum_out=ss[c][h][:])
 
@@ -101,7 +84,15 @@ def tile_attend_nrm_topk_kernel(tc, qT, k_words, k_scales, offs, out):
 
         for c in range(2):
             for h in range(2):
-                product(c, h)
+                nc.tensor.matmul_mx(
+                    out=acc[c][h][:],
+                    lhsT=q_codes[c][:].bitcast(FP8X4),
+                    lhsT_scale=q_scales[c][:],
+                    rhs=key_words[:, h * HALF : (h + 1) * HALF].bitcast(FP8X4),
+                    rhs_scale=key_scales[:, h * HALF : (h + 1) * HALF],
+                    start=True,
+                    stop=True,
+                )
 
         square(0, 0)
         nc.vector.tensor_scalar(bias[0][:], ss[0][0][:], eps[:], None, ALU.add)
@@ -114,6 +105,7 @@ def tile_attend_nrm_topk_kernel(tc, qT, k_words, k_scales, offs, out):
         nc.vector.tensor_copy(held[2][:], acc[1][0][:])
         square(1, 1)
         nc.scalar.activation(rinv[1][:], ss[1][1][:], ACT.Abs_reciprocal_sqrt, bias=bias[1][:])
+
         nc.vector.tensor_scalar(res[0][0][:], held[0][:], rinv[0][:], None, ALU.mult)
         store(0, 0, nc.sync)
         nc.vector.tensor_scalar(res[0][1][:], held[1][:], rinv[0][:], None, ALU.mult)

@@ -16,7 +16,7 @@ P = 128
 PACK = 4
 D, NQ, T, N = 512, 256, 2048, 512
 HALF = N // 2
-LEAD = 896
+LEAD = 256
 FLOPS = 2 * NQ * N * D
 
 
@@ -33,16 +33,17 @@ def tile_attend_nrm_topk_kernel(tc, qT, k_words, k_scales, offs, out):
         ones = sb.tile([P, 1], F32, name="ones")
         eps = sb.tile([P, 1], F32, name="eps")
 
-        nc.vector.memset(pool_scales[:].bitcast(I32), 0)
+        nc.scalar.dma_start(out=pool_scales[112:P, :].bitcast(I32), in_=k_scales[0].bitcast(I32))
+        nc.vector.memset(pool_scales[0:96, :].bitcast(I32), 0)
+        nc.vector.memset(pool_scales[96:112, :].bitcast(I32), 0)
         nc.vector.memset(ones[:], 1.0)
+        key_scales = sb.tile([P, N], U8, name="key_scales", align_bytes=64)
+        nc.vector.memset(key_scales[:].bitcast(I32), 0)
         nc.scalar.activation(eps[:], ones[:], ACT.Abs_reciprocal_sqrt, scale=1e8)
 
         words = k_words[0].rearrange("p t r -> p (t r)").bitcast(I32)
         nc.sync.dma_start(out=pool_words[:, 0:LEAD].bitcast(I32), in_=words[:, 0:LEAD])
         nc.sync.dma_start(offsets[:], offs)
-        scale_rows = k_scales[0].rearrange("(g r) t -> r g t", r=4)
-        for r in range(4):
-            nc.sync.dma_start(out=pool_scales[r:P:32, :].bitcast(I32), in_=scale_rows[r].bitcast(I32))
         nc.sync.dma_start(out=pool_words[:, LEAD:T].bitcast(I32), in_=words[:, LEAD:T])
         q_rows = qT[0].rearrange("(p j) w -> p j w", j=PACK)
         for c in range(2):
@@ -52,8 +53,10 @@ def tile_attend_nrm_topk_kernel(tc, qT, k_words, k_scales, offs, out):
         q_codes = [sb.tile([P, P], U32, name="q_codes%d" % c, align_bytes=64) for c in range(2)]
         q_scales = [sb.tile([P, P], U8, name="q_scales%d" % c, align_bytes=64) for c in range(2)]
 
-        key_scales = sb.tile([P, N], U8, name="key_scales", align_bytes=64)
-        nc.vector.tensor_copy(key_scales[:], pool_scales[:].indirect(offsets[:]))
+        picked_scales = sb.tile([P, N], U8, name="picked_scales", align_bytes=64)
+        nc.vector.tensor_copy(picked_scales[:], pool_scales[:].indirect(offsets[:]))
+        for r in range(4):
+            nc.scalar.dma_start(out=key_scales[r:P:32, :].bitcast(I32), in_=picked_scales[112 + r : P : 4, :].bitcast(I32))
         key_words = sb.tile([P, N], U32, name="key_words", align_bytes=64)
         nc.vector.tensor_copy(key_words[:], pool_words[:].indirect(offsets[:]))
 

@@ -16,7 +16,7 @@ P = 128
 PACK = 4
 D, NQ, T, N = 512, 256, 2048, 512
 HALF = N // 2
-LEAD = 256
+LEAD = 512
 FLOPS = 2 * NQ * N * D
 
 
@@ -33,9 +33,7 @@ def tile_attend_nrm_topk_kernel(tc, qT, k_words, k_scales, offs, out):
         ones = sb.tile([P, 1], F32, name="ones")
         eps = sb.tile([P, 1], F32, name="eps")
 
-        nc.scalar.dma_start(out=pool_scales[112:P, :].bitcast(I32), in_=k_scales[0].bitcast(I32))
-        nc.vector.memset(pool_scales[0:96, :].bitcast(I32), 0)
-        nc.vector.memset(pool_scales[96:112, :].bitcast(I32), 0)
+        nc.vector.memset(pool_scales[:].bitcast(I32), 0)
         nc.vector.memset(ones[:], 1.0)
         key_scales = sb.tile([P, N], U8, name="key_scales", align_bytes=64)
         nc.vector.memset(key_scales[:].bitcast(I32), 0)
@@ -44,6 +42,7 @@ def tile_attend_nrm_topk_kernel(tc, qT, k_words, k_scales, offs, out):
         words = k_words[0].rearrange("p t r -> p (t r)").bitcast(I32)
         nc.sync.dma_start(out=pool_words[:, 0:LEAD].bitcast(I32), in_=words[:, 0:LEAD])
         nc.sync.dma_start(offsets[:], offs)
+        nc.sync.dma_start(out=pool_scales[32:96:4, :].bitcast(I32), in_=k_scales[0].bitcast(I32))
         nc.sync.dma_start(out=pool_words[:, LEAD:T].bitcast(I32), in_=words[:, LEAD:T])
         q_rows = qT[0].rearrange("(p j) w -> p j w", j=PACK)
         for c in range(2):
@@ -56,7 +55,8 @@ def tile_attend_nrm_topk_kernel(tc, qT, k_words, k_scales, offs, out):
         picked_scales = sb.tile([P, N], U8, name="picked_scales", align_bytes=64)
         nc.vector.tensor_copy(picked_scales[:], pool_scales[:].indirect(offsets[:]))
         for r in range(4):
-            nc.scalar.dma_start(out=key_scales[r:P:32, :].bitcast(I32), in_=picked_scales[112 + r : P : 4, :].bitcast(I32))
+            queue = nc.sync if r % 2 else nc.scalar
+            queue.dma_start(out=key_scales[r:P:32, :].bitcast(I32), in_=picked_scales[32 + 4 * r : 96 : 16, :].bitcast(I32))
         key_words = sb.tile([P, N], U32, name="key_words", align_bytes=64)
         nc.vector.tensor_copy(key_words[:], pool_words[:].indirect(offsets[:]))
 

@@ -27,7 +27,10 @@ def tile_attend_nrm_topk_kernel(tc, qT, k_words, k_scales, offs, out):
         ps = ctx.enter_context(tc.psum_pool(name="ps", bufs=1))
 
         offsets = sb.tile([P, N // 16], U16, name="offsets")
-        q_raw = [sb.tile([P, PACK, P], F32, name="q_raw%d" % c) for c in range(2)]
+        q_raw = [
+            sb.tile([P, PACK, P], F32, name="q_raw0", tag="raw_then_bf", align_bytes=64),
+            sb.tile([P, PACK, P], F32, name="q_raw1"),
+        ]
         pool_scales = sb.tile([P, T], U8, name="pool_scales", align_bytes=64)
         pool_words = sb.tile([P, T], U32, name="pool_words", align_bytes=64)
         ones = sb.tile([P, 1], F32, name="ones")
@@ -48,7 +51,6 @@ def tile_attend_nrm_topk_kernel(tc, qT, k_words, k_scales, offs, out):
         for c in range(2):
             nc.sync.dma_start(out=q_raw[c][:], in_=q_rows[:, :, c * P : (c + 1) * P])
 
-        q_bf = [sb.tile([P, P, PACK], BF16, name="q_bf%d" % c, align_bytes=64) for c in range(2)]
         q_codes = [sb.tile([P, P], U32, name="q_codes%d" % c, align_bytes=64) for c in range(2)]
         q_scales = [sb.tile([P, P], U8, name="q_scales%d" % c, align_bytes=64) for c in range(2)]
 
@@ -60,16 +62,29 @@ def tile_attend_nrm_topk_kernel(tc, qT, k_words, k_scales, offs, out):
         key_words = sb.tile([P, N], U32, name="key_words", align_bytes=64)
         nc.vector.tensor_copy(key_words[:], pool_words[:].indirect(offsets[:]))
 
-        for c in range(2):
-            nc.scalar.copy(
-                out=q_bf[c][:].rearrange("p (g i) j -> p g j i", i=4),
-                in_=q_raw[c][:].rearrange("p j (g i) -> p g j i", i=4),
+        def interleave(copy, dst, c, lo, hi):
+            copy(
+                out=dst[:].rearrange("p (g i) j -> p g j i", i=4),
+                in_=q_raw[c][:, :, lo:hi].rearrange("p j (g i) -> p g j i", i=4),
             )
+
+        def quantise(src, c, lo, hi):
             nc.vector.quantize_mx(
-                out=q_codes[c][:].bitcast(FP8X4),
-                scales=q_scales[c][:],
-                in_=q_bf[c][:].rearrange("p w j -> p (w j)"),
+                out=q_codes[c][:, lo:hi].bitcast(FP8X4),
+                scales=q_scales[c][:, lo:hi],
+                in_=src[:].rearrange("p w j -> p (w j)"),
             )
+
+        for lo in (0, P // 2):
+            bf_0 = sb.tile([P, P // 2, PACK], BF16, name="bf_0_%d" % lo, align_bytes=64)
+            interleave(nc.scalar.copy, bf_0, 0, lo, lo + P // 2)
+            quantise(bf_0, 0, lo, lo + P // 2)
+        bf_1a = sb.tile([P, P // 2, PACK], BF16, name="bf_1a", align_bytes=64)
+        bf_1b = sb.tile([P, P // 2, PACK], BF16, name="bf_1b", tag="raw_then_bf", align_bytes=64)
+        interleave(nc.scalar.copy, bf_1a, 1, 0, P // 2)
+        interleave(nc.vector.tensor_copy, bf_1b, 1, P // 2, P)
+        quantise(bf_1a, 1, 0, P // 2)
+        quantise(bf_1b, 1, P // 2, P)
 
         acc = [[ps.tile([P, HALF], F32, name="acc%d%d" % (c, h)) for h in range(2)] for c in range(2)]
         squares = [sb.tile([P, HALF], BF16, name="squares%d" % i) for i in range(4)]

@@ -131,4 +131,4 @@ def tile_attend_nrm_topk_kernel(tc, qT, k_words, k_scales, offs, out):
         nc.vector.tensor_scalar(res[1][0][:], held[2][:], rinv[1][:], None, ALU.mult)
         store(1, 0, nc.sync)
         nc.scalar.activation(res[1][1][:], acc[1][1][:], ACT.Copy, scale=rinv[1][:])
-        store(1, 1, nc.scalar)
+        store(1, 1, nc.sync)

@@ -15,6 +15,7 @@ ALU = mybir.AluOpType
 P = 128
 PACK = 4
 D, NQ, T, N = 512, 256, 2048, 512
+PIECE = P // 2
 HALF = N // 2
 LEAD = 512
 FLOPS = 2 * NQ * N * D
@@ -27,10 +28,9 @@ def tile_attend_nrm_topk_kernel(tc, qT, k_words, k_scales, offs, out):
         ps = ctx.enter_context(tc.psum_pool(name="ps", bufs=1))
 
         offsets = sb.tile([P, N // 16], U16, name="offsets")
-        q_raw = [
-            sb.tile([P, PACK, P], F32, name="q_raw0", tag="raw_then_bf", align_bytes=64),
-            sb.tile([P, PACK, P], F32, name="q_raw1"),
-        ]
+        raw_0a = sb.tile([P, 2, P], F32, name="raw_0a")
+        raw_0b = sb.tile([P, 2, P], F32, name="raw_0b", tag="raw_then_bf", align_bytes=64)
+        raw_1 = sb.tile([P, PACK, P], F32, name="raw_1")
         pool_scales = sb.tile([P, T], U8, name="pool_scales", align_bytes=64)
         pool_words = sb.tile([P, T], U32, name="pool_words", align_bytes=64)
         ones = sb.tile([P, 1], F32, name="ones")
@@ -48,8 +48,9 @@ def tile_attend_nrm_topk_kernel(tc, qT, k_words, k_scales, offs, out):
         nc.sync.dma_start(out=pool_scales[32:96:4, :].bitcast(I32), in_=k_scales[0].bitcast(I32))
         nc.sync.dma_start(out=pool_words[:, LEAD:T].bitcast(I32), in_=words[:, LEAD:T])
         q_rows = qT[0].rearrange("(p j) w -> p j w", j=PACK)
-        for c in range(2):
-            nc.sync.dma_start(out=q_raw[c][:], in_=q_rows[:, :, c * P : (c + 1) * P])
+        nc.sync.dma_start(out=raw_0a[:], in_=q_rows[:, 0:2, 0:P])
+        nc.sync.dma_start(out=raw_0b[:], in_=q_rows[:, 2:PACK, 0:P])
+        nc.sync.dma_start(out=raw_1[:], in_=q_rows[:, :, P:NQ])
 
         q_codes = [sb.tile([P, P], U32, name="q_codes%d" % c, align_bytes=64) for c in range(2)]
         q_scales = [sb.tile([P, P], U8, name="q_scales%d" % c, align_bytes=64) for c in range(2)]
@@ -62,29 +63,30 @@ def tile_attend_nrm_topk_kernel(tc, qT, k_words, k_scales, offs, out):
         key_words = sb.tile([P, N], U32, name="key_words", align_bytes=64)
         nc.vector.tensor_copy(key_words[:], pool_words[:].indirect(offsets[:]))
 
-        def interleave(copy, dst, c, lo, hi):
+        def interleave(copy, dst, src):
             copy(
-                out=dst[:].rearrange("p (g i) j -> p g j i", i=4),
-                in_=q_raw[c][:, :, lo:hi].rearrange("p j (g i) -> p g j i", i=4),
+                out=dst.rearrange("p (g i) j -> p g j i", i=4),
+                in_=src.rearrange("p j (g i) -> p g j i", i=4),
             )
 
         def quantise(src, c, lo, hi):
             nc.vector.quantize_mx(
                 out=q_codes[c][:, lo:hi].bitcast(FP8X4),
                 scales=q_scales[c][:, lo:hi],
-                in_=src[:].rearrange("p w j -> p (w j)"),
+                in_=src.rearrange("p w j -> p (w j)"),
             )
 
-        for lo in (0, P // 2):
-            bf_0 = sb.tile([P, P // 2, PACK], BF16, name="bf_0_%d" % lo, align_bytes=64)
-            interleave(nc.scalar.copy, bf_0, 0, lo, lo + P // 2)
-            quantise(bf_0, 0, lo, lo + P // 2)
+        bf_0 = sb.tile([P, P, PACK], BF16, name="bf_0", align_bytes=64)
+        interleave(nc.scalar.copy, bf_0[:, :, 0:2], raw_0a[:])
+        for lo in (0, PIECE):
+            interleave(nc.scalar.copy, bf_0[:, lo : lo + PIECE, 2:PACK], raw_0b[:, :, lo : lo + PIECE])
+            quantise(bf_0[:, lo : lo + PIECE, :], 0, lo, lo + PIECE)
         bf_1a = sb.tile([P, P // 2, PACK], BF16, name="bf_1a", align_bytes=64)
         bf_1b = sb.tile([P, P // 2, PACK], BF16, name="bf_1b", tag="raw_then_bf", align_bytes=64)
-        interleave(nc.scalar.copy, bf_1a, 1, 0, P // 2)
-        interleave(nc.vector.tensor_copy, bf_1b, 1, P // 2, P)
-        quantise(bf_1a, 1, 0, P // 2)
-        quantise(bf_1b, 1, P // 2, P)
+        interleave(nc.scalar.copy, bf_1a[:], raw_1[:, :, 0:PIECE])
+        interleave(nc.vector.tensor_copy, bf_1b[:], raw_1[:, :, PIECE:P])
+        quantise(bf_1a[:], 1, 0, P // 2)
+        quantise(bf_1b[:], 1, P // 2, P)
 
         acc = [[ps.tile([P, HALF], F32, name="acc%d%d" % (c, h)) for h in range(2)] for c in range(2)]
         squares = [sb.tile([P, HALF], BF16, name="squares%d" % i) for i in range(4)]

@@ -17,7 +17,7 @@ PACK = 4
 D, NQ, T, N = 512, 256, 2048, 512
 PIECE = P // 2
 HALF = N // 2
-LEAD = 512
+FIRST = 384
 FLOPS = 2 * NQ * N * D
 
 
@@ -36,19 +36,19 @@ def tile_attend_nrm_topk_kernel(tc, qT, k_words, k_scales, offs, out):
         ones = sb.tile([P, 1], F32, name="ones")
         eps = sb.tile([P, 1], F32, name="eps")
 
-        nc.vector.memset(pool_scales[:].bitcast(I32), 0)
+        nc.vector.memset(pool_scales[0:96, :].bitcast(I32), 0)
+        nc.vector.memset(pool_scales[96:112, :].bitcast(I32), 0)
         nc.vector.memset(ones[:], 1.0)
         key_scales = sb.tile([P, N], U8, name="key_scales", align_bytes=64)
         nc.vector.memset(key_scales[:].bitcast(I32), 0)
         nc.scalar.activation(eps[:], ones[:], ACT.Abs_reciprocal_sqrt, scale=1e8)
 
         words = k_words[0].rearrange("p t r -> p (t r)").bitcast(I32)
-        nc.sync.dma_start(out=pool_words[:, 0:LEAD].bitcast(I32), in_=words[:, 0:LEAD])
-        nc.sync.dma_start(offsets[:], offs)
-        nc.sync.dma_start(out=pool_scales[32:96:4, :].bitcast(I32), in_=k_scales[0].bitcast(I32))
-        nc.sync.dma_start(out=pool_words[:, LEAD:T].bitcast(I32), in_=words[:, LEAD:T])
         q_rows = qT[0].rearrange("(p j) w -> p j w", j=PACK)
         nc.sync.dma_start(out=raw_0a[:], in_=q_rows[:, 0:2, 0:P])
+        nc.sync.dma_start(offsets[:], offs)
+        nc.sync.dma_start(out=pool_scales[112:P, :].bitcast(I32), in_=k_scales[0].bitcast(I32))
+        nc.sync.dma_start(out=pool_words[:].bitcast(I32), in_=words)
         nc.sync.dma_start(out=raw_0b[:], in_=q_rows[:, 2:PACK, 0:P])
         nc.sync.dma_start(out=raw_1[:], in_=q_rows[:, :, P:NQ])
 
@@ -59,9 +59,9 @@ def tile_attend_nrm_topk_kernel(tc, qT, k_words, k_scales, offs, out):
         nc.vector.tensor_copy(picked_scales[:], pool_scales[:].indirect(offsets[:]))
         for r in range(4):
             queue = nc.sync if r % 2 else nc.scalar
-            queue.dma_start(out=key_scales[r:P:32, :].bitcast(I32), in_=picked_scales[32 + 4 * r : 96 : 16, :].bitcast(I32))
-        key_words = sb.tile([P, N], U32, name="key_words", align_bytes=64)
-        nc.vector.tensor_copy(key_words[:], pool_words[:].indirect(offsets[:]))
+            queue.dma_start(out=key_scales[r:P:32, :].bitcast(I32), in_=picked_scales[112 + r : P : 4, :].bitcast(I32))
+        keys_first = sb.tile([P, FIRST], U32, name="keys_first", align_bytes=64)
+        nc.vector.tensor_copy(keys_first[:], pool_words[:].indirect(offsets[:, 0 : FIRST // 16]))
 
         def interleave(copy, dst, src):
             copy(
@@ -76,7 +76,7 @@ def tile_attend_nrm_topk_kernel(tc, qT, k_words, k_scales, offs, out):
                 in_=src.rearrange("p w j -> p (w j)"),
             )
 
-        bf_0 = sb.tile([P, P, PACK], BF16, name="bf_0", align_bytes=64)
+        bf_0 = sb.tile([P, P, PACK], BF16, name="bf_0", tag="bf_then_keys", align_bytes=64)
         interleave(nc.scalar.copy, bf_0[:, :, 0:2], raw_0a[:])
         for lo in (0, PIECE):
             interleave(nc.scalar.copy, bf_0[:, lo : lo + PIECE, 2:PACK], raw_0b[:, :, lo : lo + PIECE])
@@ -85,6 +85,8 @@ def tile_attend_nrm_topk_kernel(tc, qT, k_words, k_scales, offs, out):
         bf_1b = sb.tile([P, P // 2, PACK], BF16, name="bf_1b", tag="raw_then_bf", align_bytes=64)
         interleave(nc.scalar.copy, bf_1a[:], raw_1[:, :, 0:PIECE])
         interleave(nc.vector.tensor_copy, bf_1b[:], raw_1[:, :, PIECE:P])
+        keys_last = sb.tile([P, N - FIRST], U32, name="keys_last", tag="bf_then_keys", align_bytes=64)
+        nc.vector.tensor_copy(keys_last[:], pool_words[:].indirect(offsets[:, FIRST // 16 : N // 16]))
         quantise(bf_1a[:], 1, 0, P // 2)
         quantise(bf_1b[:], 1, P // 2, P)
 
@@ -103,13 +105,13 @@ def tile_attend_nrm_topk_kernel(tc, qT, k_words, k_scales, offs, out):
             engine.dma_start(out=out[0, c * P : (c + 1) * P, h * HALF : (h + 1) * HALF], in_=res[c][h][:])
 
         for c in range(2):
-            for h in range(2):
+            for lo, hi, keys in ((0, HALF, keys_first[:, 0:HALF]), (HALF, FIRST, keys_first[:, HALF:FIRST]), (FIRST, N, keys_last[:])):
                 nc.tensor.matmul_mx(
-                    out=acc[c][h][:],
+                    out=acc[c][lo // HALF][:, lo % HALF : lo % HALF + hi - lo],
                     lhsT=q_codes[c][:].bitcast(FP8X4),
                     lhsT_scale=q_scales[c][:],
-                    rhs=key_words[:, h * HALF : (h + 1) * HALF].bitcast(FP8X4),
-                    rhs_scale=key_scales[:, h * HALF : (h + 1) * HALF],
+                    rhs=keys.bitcast(FP8X4),
+                    rhs_scale=key_scales[:, lo:hi],
                     start=True,
                     stop=True,
                 )

@@ -18,6 +18,7 @@ D, NQ, T, N = 512, 256, 2048, 512
 PIECE = P // 2
 HALF = N // 2
 FIRST = 384
+LEAD = 256
 FLOPS = 2 * NQ * N * D
 
 
@@ -36,8 +37,7 @@ def tile_attend_nrm_topk_kernel(tc, qT, k_words, k_scales, offs, out):
         ones = sb.tile([P, 1], F32, name="ones")
         eps = sb.tile([P, 1], F32, name="eps")
 
-        nc.vector.memset(pool_scales[0:96, :].bitcast(I32), 0)
-        nc.vector.memset(pool_scales[96:112, :].bitcast(I32), 0)
+        nc.vector.memset(pool_scales[:].bitcast(I32), 0)
         nc.vector.memset(ones[:], 1.0)
         key_scales = sb.tile([P, N], U8, name="key_scales", align_bytes=64)
         nc.vector.memset(key_scales[:].bitcast(I32), 0)
@@ -47,8 +47,9 @@ def tile_attend_nrm_topk_kernel(tc, qT, k_words, k_scales, offs, out):
         q_rows = qT[0].rearrange("(p j) w -> p j w", j=PACK)
         nc.sync.dma_start(out=raw_0a[:], in_=q_rows[:, 0:2, 0:P])
         nc.sync.dma_start(offsets[:], offs)
-        nc.sync.dma_start(out=pool_scales[112:P, :].bitcast(I32), in_=k_scales[0].bitcast(I32))
-        nc.sync.dma_start(out=pool_words[:].bitcast(I32), in_=words)
+        nc.sync.dma_start(out=pool_words[:, 0:LEAD].bitcast(I32), in_=words[:, 0:LEAD])
+        nc.sync.dma_start(out=pool_scales[32:96:4, :].bitcast(I32), in_=k_scales[0].bitcast(I32))
+        nc.sync.dma_start(out=pool_words[:, LEAD:T].bitcast(I32), in_=words[:, LEAD:T])
         nc.sync.dma_start(out=raw_0b[:], in_=q_rows[:, 2:PACK, 0:P])
         nc.sync.dma_start(out=raw_1[:], in_=q_rows[:, :, P:NQ])
 
@@ -59,7 +60,7 @@ def tile_attend_nrm_topk_kernel(tc, qT, k_words, k_scales, offs, out):
         nc.vector.tensor_copy(picked_scales[:], pool_scales[:].indirect(offsets[:]))
         for r in range(4):
             queue = nc.sync if r % 2 else nc.scalar
-            queue.dma_start(out=key_scales[r:P:32, :].bitcast(I32), in_=picked_scales[112 + r : P : 4, :].bitcast(I32))
+            queue.dma_start(out=key_scales[r:P:32, :].bitcast(I32), in_=picked_scales[32 + 4 * r : 96 : 16, :].bitcast(I32))
         keys_first = sb.tile([P, FIRST], U32, name="keys_first", align_bytes=64)
         nc.vector.tensor_copy(keys_first[:], pool_words[:].indirect(offsets[:, 0 : FIRST // 16]))
 

@@ -97,13 +97,13 @@ def tile_attend_nrm_topk_kernel(tc, qT, k_words, k_scales, offs, out):
         bias = [sb.tile([P, 1], F32, name="bias%d" % c) for c in range(2)]
         rinv = [sb.tile([P, 1], F32, name="rinv%d" % c) for c in range(2)]
         held = [sb.tile([P, HALF], F32, name="held%d" % i) for i in range(3)]
-        res = [[sb.tile([P, HALF], F32, name="res%d%d" % (c, h)) for h in range(2)] for c in range(2)]
+        res = [sb.tile([P, N], F32, name="res%d" % c) for c in range(2)]
 
         def square(c, h):
             nc.scalar.activation(squares[2 * c + h][:], acc[c][h][:], ACT.Square, accum_out=ss[c][h][:])
 
-        def store(c, h, engine):
-            engine.dma_start(out=out[0, c * P : (c + 1) * P, h * HALF : (h + 1) * HALF], in_=res[c][h][:])
+        def store(c, lo, hi):
+            nc.sync.dma_start(out=out[0, c * P : (c + 1) * P, lo:hi], in_=res[c][:, lo:hi])
 
         for c in range(2):
             for lo, hi, keys in ((0, HALF, keys_first[:, 0:HALF]), (HALF, FIRST, keys_first[:, HALF:FIRST]), (FIRST, N, keys_last[:])):
@@ -129,11 +129,10 @@ def tile_attend_nrm_topk_kernel(tc, qT, k_words, k_scales, offs, out):
         square(1, 1)
         nc.scalar.activation(rinv[1][:], ss[1][1][:], ACT.Abs_reciprocal_sqrt, bias=bias[1][:])
 
-        nc.vector.tensor_scalar(res[0][0][:], held[0][:], rinv[0][:], None, ALU.mult)
-        store(0, 0, nc.sync)
-        nc.vector.tensor_scalar(res[0][1][:], held[1][:], rinv[0][:], None, ALU.mult)
-        store(0, 1, nc.sync)
-        nc.vector.tensor_scalar(res[1][0][:], held[2][:], rinv[1][:], None, ALU.mult)
-        store(1, 0, nc.sync)
-        nc.scalar.activation(res[1][1][:], acc[1][1][:], ACT.Copy, scale=rinv[1][:])
-        store(1, 1, nc.sync)
+        nc.vector.tensor_scalar(res[0][:, 0:HALF], held[0][:], rinv[0][:], None, ALU.mult)
+        store(0, 0, HALF)
+        nc.vector.tensor_scalar(res[0][:, HALF:N], held[1][:], rinv[0][:], None, ALU.mult)
+        store(0, HALF, N)
+        nc.vector.tensor_scalar(res[1][:, 0:HALF], held[2][:], rinv[1][:], None, ALU.mult)
+        nc.scalar.activation(res[1][:, HALF:N], acc[1][1][:], ACT.Copy, scale=rinv[1][:])
+        store(1, 0, N)

@@ -15,10 +15,9 @@ ALU = mybir.AluOpType
 P = 128
 PACK = 4
 D, NQ, T, N = 512, 256, 2048, 512
-PIECE = P // 2
 HALF = N // 2
-FIRST = 384
-LEAD = 256
+PIECE = P // 2
+LAST = 128
 FLOPS = 2 * NQ * N * D
 
 
@@ -29,70 +28,80 @@ def tile_attend_nrm_topk_kernel(tc, qT, k_words, k_scales, offs, out):
         ps = ctx.enter_context(tc.psum_pool(name="ps", bufs=1))
 
         offsets = sb.tile([P, N // 16], U16, name="offsets")
-        raw_0a = sb.tile([P, 2, P], F32, name="raw_0a")
-        raw_0b = sb.tile([P, 2, P], F32, name="raw_0b", tag="raw_then_bf", align_bytes=64)
-        raw_1 = sb.tile([P, PACK, P], F32, name="raw_1")
-        pool_scales = sb.tile([P, T], U8, name="pool_scales", align_bytes=64)
+        raw_0 = sb.tile([P, PACK, P], F32, name="raw_0")
+        raw_1 = sb.tile([P, PACK, P], F32, name="raw_1", tag="raw_then_squares")
+        pool_scales = sb.tile([P, T], U8, name="pool_scales", tag="scales_then_codes", align_bytes=64)
         pool_words = sb.tile([P, T], U32, name="pool_words", align_bytes=64)
+        key_scales = sb.tile([P, N], U8, name="key_scales", align_bytes=64)
         ones = sb.tile([P, 1], F32, name="ones")
         eps = sb.tile([P, 1], F32, name="eps")
 
         nc.vector.memset(pool_scales[:].bitcast(I32), 0)
         nc.vector.memset(ones[:], 1.0)
-        key_scales = sb.tile([P, N], U8, name="key_scales", align_bytes=64)
         nc.vector.memset(key_scales[:].bitcast(I32), 0)
         nc.scalar.activation(eps[:], ones[:], ACT.Abs_reciprocal_sqrt, scale=1e8)
 
         words = k_words[0].rearrange("p t r -> p (t r)").bitcast(I32)
         q_rows = qT[0].rearrange("(p j) w -> p j w", j=PACK)
-        nc.sync.dma_start(out=raw_0a[:], in_=q_rows[:, 0:2, 0:P])
+        nc.sync.dma_start(out=raw_0[:], in_=q_rows[:, :, 0:P])
         nc.sync.dma_start(offsets[:], offs)
-        nc.sync.dma_start(out=pool_words[:, 0:LEAD].bitcast(I32), in_=words[:, 0:LEAD])
         nc.sync.dma_start(out=pool_scales[32:96:4, :].bitcast(I32), in_=k_scales[0].bitcast(I32))
-        nc.sync.dma_start(out=pool_words[:, LEAD:T].bitcast(I32), in_=words[:, LEAD:T])
-        nc.sync.dma_start(out=raw_0b[:], in_=q_rows[:, 2:PACK, 0:P])
+        nc.sync.dma_start(out=pool_words[:].bitcast(I32), in_=words)
         nc.sync.dma_start(out=raw_1[:], in_=q_rows[:, :, P:NQ])
-
-        q_codes = [sb.tile([P, P], U32, name="q_codes%d" % c, align_bytes=64) for c in range(2)]
-        q_scales = [sb.tile([P, P], U8, name="q_scales%d" % c, align_bytes=64) for c in range(2)]
 
         picked_scales = sb.tile([P, N], U8, name="picked_scales", align_bytes=64)
         nc.vector.tensor_copy(picked_scales[:], pool_scales[:].indirect(offsets[:]))
-        for r in range(4):
-            queue = nc.sync if r % 2 else nc.scalar
-            queue.dma_start(out=key_scales[r:P:32, :].bitcast(I32), in_=picked_scales[32 + 4 * r : 96 : 16, :].bitcast(I32))
-        keys_first = sb.tile([P, FIRST], U32, name="keys_first", align_bytes=64)
-        nc.vector.tensor_copy(keys_first[:], pool_words[:].indirect(offsets[:, 0 : FIRST // 16]))
 
-        def interleave(copy, dst, src):
-            copy(
+        def interleave(dst, src):
+            nc.scalar.copy(
                 out=dst.rearrange("p (g i) j -> p g j i", i=4),
                 in_=src.rearrange("p j (g i) -> p g j i", i=4),
             )
 
-        def quantise(src, c, lo, hi):
+        def quantise(c, lo, hi, src):
             nc.vector.quantize_mx(
                 out=q_codes[c][:, lo:hi].bitcast(FP8X4),
                 scales=q_scales[c][:, lo:hi],
                 in_=src.rearrange("p w j -> p (w j)"),
             )
 
-        bf_0 = sb.tile([P, P, PACK], BF16, name="bf_0", tag="bf_then_keys", align_bytes=64)
-        interleave(nc.scalar.copy, bf_0[:, :, 0:2], raw_0a[:])
+        q_codes = [
+            sb.tile([P, P], U32, name="q_codes0", tag="scales_then_codes", align_bytes=64),
+            sb.tile([P, P], U32, name="q_codes1", align_bytes=64),
+        ]
+        q_scales = [sb.tile([P, P], U8, name="q_scales%d" % c, align_bytes=64) for c in range(2)]
+        grouped_0 = sb.tile([P, P, PACK], BF16, name="grouped_0", align_bytes=64)
+        interleave(grouped_0[:], raw_0[:])
+        for r in range(4):
+            queue = nc.sync if r % 2 else nc.scalar
+            queue.dma_start(out=key_scales[r:P:32, :].bitcast(I32), in_=picked_scales[32 + 4 * r : 96 : 16, :].bitcast(I32))
+        quantise(0, 0, P, grouped_0[:])
+
+        keys = [sb.tile([P, HALF], U32, name="keys%d" % h, align_bytes=64) for h in range(2)]
+        for lo, hi in ((0, HALF), (HALF, N - LAST), (N - LAST, N)):
+            nc.vector.tensor_copy(
+                keys[lo // HALF][:, lo % HALF : lo % HALF + hi - lo], pool_words[:].indirect(offsets[:, lo // 16 : hi // 16])
+            )
         for lo in (0, PIECE):
-            interleave(nc.scalar.copy, bf_0[:, lo : lo + PIECE, 2:PACK], raw_0b[:, :, lo : lo + PIECE])
-            quantise(bf_0[:, lo : lo + PIECE, :], 0, lo, lo + PIECE)
-        bf_1a = sb.tile([P, P // 2, PACK], BF16, name="bf_1a", align_bytes=64)
-        bf_1b = sb.tile([P, P // 2, PACK], BF16, name="bf_1b", tag="raw_then_bf", align_bytes=64)
-        interleave(nc.scalar.copy, bf_1a[:], raw_1[:, :, 0:PIECE])
-        interleave(nc.vector.tensor_copy, bf_1b[:], raw_1[:, :, PIECE:P])
-        keys_last = sb.tile([P, N - FIRST], U32, name="keys_last", tag="bf_then_keys", align_bytes=64)
-        nc.vector.tensor_copy(keys_last[:], pool_words[:].indirect(offsets[:, FIRST // 16 : N // 16]))
-        quantise(bf_1a[:], 1, 0, P // 2)
-        quantise(bf_1b[:], 1, P // 2, P)
+            grouped_1 = sb.tile([P, PIECE, PACK], BF16, name="grouped_1_%d" % lo, align_bytes=64)
+            interleave(grouped_1[:], raw_1[:, :, lo : lo + PIECE])
+            quantise(1, lo, lo + PIECE, grouped_1[:])
 
         acc = [[ps.tile([P, HALF], F32, name="acc%d%d" % (c, h)) for h in range(2)] for c in range(2)]
-        squares = [sb.tile([P, HALF], BF16, name="squares%d" % i) for i in range(4)]
+        for c, lo, hi in ((0, 0, HALF), (0, HALF, N - LAST), (0, N - LAST, N), (1, 0, HALF), (1, HALF, N)):
+            h, cols = lo // HALF, slice(lo % HALF, lo % HALF + hi - lo)
+            nc.tensor.matmul_mx(
+                out=acc[c][h][:, cols],
+                lhsT=q_codes[c][:].bitcast(FP8X4),
+                lhsT_scale=q_scales[c][:],
+                rhs=keys[h][:, cols].bitcast(FP8X4),
+                rhs_scale=key_scales[:, lo:hi],
+                start=True,
+                stop=True,
+            )
+
+        squares = [sb.tile([P, HALF], BF16, name="squares0", tag="raw_then_squares")]
+        squares.extend(sb.tile([P, HALF], BF16, name="squares%d" % i) for i in range(1, 4))
         ss = [[sb.tile([P, 1], F32, name="ss%d%d" % (c, h)) for h in range(2)] for c in range(2)]
         bias = [sb.tile([P, 1], F32, name="bias%d" % c) for c in range(2)]
         rinv = [sb.tile([P, 1], F32, name="rinv%d" % c) for c in range(2)]
@@ -104,18 +113,6 @@ def tile_attend_nrm_topk_kernel(tc, qT, k_words, k_scales, offs, out):
 
         def store(c, lo, hi):
             nc.sync.dma_start(out=out[0, c * P : (c + 1) * P, lo:hi], in_=res[c][:, lo:hi])
-
-        for c in range(2):
-            for lo, hi, keys in ((0, HALF, keys_first[:, 0:HALF]), (HALF, FIRST, keys_first[:, HALF:FIRST]), (FIRST, N, keys_last[:])):
-                nc.tensor.matmul_mx(
-                    out=acc[c][lo // HALF][:, lo % HALF : lo % HALF + hi - lo],
-                    lhsT=q_codes[c][:].bitcast(FP8X4),
-                    lhsT_scale=q_scales[c][:],
-                    rhs=keys.bitcast(FP8X4),
-                    rhs_scale=key_scales[:, lo:hi],
-                    start=True,
-                    stop=True,
-                )
 
         square(0, 0)
         nc.vector.tensor_scalar(bias[0][:], ss[0][0][:], eps[:], None, ALU.add)

@@ -18,6 +18,8 @@ D, NQ, T, N = 512, 256, 2048, 512
 HALF = N // 2
 PIECE = P // 2
 LAST = 128
+COUNT = HALF // 2
+LINE = 4
 FLOPS = 2 * NQ * N * D
 
 
@@ -33,13 +35,15 @@ def tile_attend_nrm_topk_kernel(tc, qT, k_words, k_scales, offs, out):
         pool_scales = sb.tile([P, T], U8, name="pool_scales", tag="scales_then_codes", align_bytes=64)
         pool_words = sb.tile([P, T], U32, name="pool_words", align_bytes=64)
         key_scales = sb.tile([P, N], U8, name="key_scales", align_bytes=64)
-        ones = sb.tile([P, 1], F32, name="ones")
-        eps = sb.tile([P, 1], F32, name="eps")
+        stats = sb.tile([P, 3, 6], F32, name="stats")
+        flat = stats[:].rearrange("p g s -> p (g s)")
+        eps = stats[:, 0, 0:1]
 
         nc.vector.memset(pool_scales[:].bitcast(I32), 0)
-        nc.vector.memset(ones[:], 1.0)
+        nc.vector.memset(stats[:], 1.0 / COUNT)
+        nc.vector.memset(stats[:, 2, 2:3], 0.0)
         nc.vector.memset(key_scales[:].bitcast(I32), 0)
-        nc.scalar.activation(eps[:], ones[:], ACT.Abs_reciprocal_sqrt, scale=1e8)
+        nc.scalar.activation(flat[:, 0:17:16], flat[:, 1:4:2], ACT.Abs_reciprocal_sqrt, scale=1e8 * COUNT)
 
         words = k_words[0].rearrange("p t r -> p (t r)").bitcast(I32)
         q_rows = qT[0].rearrange("(p j) w -> p j w", j=PACK)
@@ -100,36 +104,38 @@ def tile_attend_nrm_topk_kernel(tc, qT, k_words, k_scales, offs, out):
                 stop=True,
             )
 
-        squares = [sb.tile([P, HALF], BF16, name="squares0", tag="raw_then_squares")]
-        squares.extend(sb.tile([P, HALF], BF16, name="squares%d" % i) for i in range(1, 4))
-        ss = [[sb.tile([P, 1], F32, name="ss%d%d" % (c, h)) for h in range(2)] for c in range(2)]
+        first_squares = sb.tile([P, HALF], BF16, name="first_squares", tag="raw_then_squares")
+        later_squares = sb.tile([P, HALF + LINE], F32, name="later_squares")
+        squares = {(0, 0): first_squares[:], (0, 1): later_squares[:, 0:HALF], (1, 1): later_squares[:, LINE : HALF + LINE]}
+        last = [sb.tile([P, 1], F32, name="ss%d" % c) for c in range(2)]
+        ss = {(0, 0): later_squares[:, HALF : HALF + 1], (0, 1): last[0][:], (1, 1): last[1][:]}
         bias = [sb.tile([P, 1], F32, name="bias%d" % c) for c in range(2)]
         rinv = [sb.tile([P, 1], F32, name="rinv%d" % c) for c in range(2)]
-        held = [sb.tile([P, HALF], F32, name="held%d" % i) for i in range(3)]
+        held = sb.tile([P, HALF], F32, name="held")
+        terms = sb.tile([P, 3, 2], F32, name="terms")
         res = [sb.tile([P, N], F32, name="res%d" % c) for c in range(2)]
 
         def square(c, h):
-            nc.scalar.activation(squares[2 * c + h][:], acc[c][h][:], ACT.Square, accum_out=ss[c][h][:])
+            nc.scalar.activation(squares[c, h], acc[c][h][:], ACT.Square, accum_out=ss[c, h])
 
         def store(c, lo, hi):
             nc.sync.dma_start(out=out[0, c * P : (c + 1) * P, lo:hi], in_=res[c][:, lo:hi])
 
         square(0, 0)
-        nc.vector.tensor_scalar(bias[0][:], ss[0][0][:], eps[:], None, ALU.add)
-        nc.vector.tensor_copy(held[0][:], acc[0][0][:])
+        nc.vector.tensor_scalar(bias[0][:], ss[0, 0], eps, None, ALU.add)
+        nc.vector.tensor_copy(held[:], acc[0][0][:])
         square(0, 1)
-        nc.vector.tensor_copy(held[1][:], acc[0][1][:])
-        nc.scalar.activation(rinv[0][:], ss[0][1][:], ACT.Abs_reciprocal_sqrt, bias=bias[0][:])
-        square(1, 0)
-        nc.vector.tensor_scalar(bias[1][:], ss[1][0][:], eps[:], None, ALU.add)
-        nc.vector.tensor_copy(held[2][:], acc[1][0][:])
+        nc.scalar.activation(rinv[0][:], ss[0, 1], ACT.Abs_reciprocal_sqrt, bias=bias[0][:])
+        nc.vector.bn_stats(flat[:, 0:12:2], acc[1][0][:])
         square(1, 1)
-        nc.scalar.activation(rinv[1][:], ss[1][1][:], ACT.Abs_reciprocal_sqrt, bias=bias[1][:])
-
-        nc.vector.tensor_scalar(res[0][:, 0:HALF], held[0][:], rinv[0][:], None, ALU.mult)
+        nc.vector.tensor_scalar(res[0][:, 0:HALF], held[:], rinv[0][:], None, ALU.mult)
         store(0, 0, HALF)
-        nc.vector.tensor_scalar(res[0][:, HALF:N], held[1][:], rinv[0][:], None, ALU.mult)
+        nc.vector.scalar_tensor_tensor(
+            terms[:], stats[:, :, 2:6:2], float(COUNT), stats[:, :, 2:4], ALU.mult, ALU.mult, accum_out=bias[1][:]
+        )
+        nc.vector.tensor_scalar(res[0][:, HALF:N], acc[0][1][:], rinv[0][:], None, ALU.mult)
         store(0, HALF, N)
-        nc.vector.tensor_scalar(res[1][:, 0:HALF], held[2][:], rinv[1][:], None, ALU.mult)
+        nc.scalar.activation(rinv[1][:], ss[1, 1], ACT.Abs_reciprocal_sqrt, bias=bias[1][:])
+        nc.vector.tensor_scalar(res[1][:, 0:HALF], acc[1][0][:], rinv[1][:], None, ALU.mult)
         nc.scalar.activation(res[1][:, HALF:N], acc[1][1][:], ACT.Copy, scale=rinv[1][:])
         store(1, 0, N)

from contextlib import ExitStack

import concourse.mybir as mybir

F32 = mybir.dt.float32
BF16 = mybir.dt.bfloat16
I32 = mybir.dt.int32
U32 = mybir.dt.uint32
U16 = mybir.dt.uint16
U8 = mybir.dt.uint8
FP8X4 = mybir.dt.float8_e4m3fn_x4
ACT = mybir.ActivationFunctionType
ALU = mybir.AluOpType

P = 128
PACK = 4
D, NQ, T, N = 512, 256, 2048, 512
HALF = N // 2
PIECE = P // 2
LAST = 128
COUNT = HALF // 2
LINE = 4
FLOPS = 2 * NQ * N * D


def tile_attend_nrm_topk_kernel(tc, qT, k_words, k_scales, offs, out):
    nc = tc.nc
    with ExitStack() as ctx:
        sb = ctx.enter_context(tc.tile_pool(name="sb", bufs=1))
        ps = ctx.enter_context(tc.psum_pool(name="ps", bufs=1))

        offsets = sb.tile([P, N // 16], U16, name="offsets")
        raw_0 = sb.tile([P, PACK, P], F32, name="raw_0")
        raw_1 = sb.tile([P, PACK, P], F32, name="raw_1", tag="raw_then_squares")
        pool_scales = sb.tile([P, T], U8, name="pool_scales", tag="scales_then_codes", align_bytes=64)
        pool_words = sb.tile([P, T], U32, name="pool_words", align_bytes=64)
        key_scales = sb.tile([P, N], U8, name="key_scales", align_bytes=64)
        stats = sb.tile([P, 3, 6], F32, name="stats")
        flat = stats[:].rearrange("p g s -> p (g s)")
        eps = stats[:, 0, 0:1]

        nc.vector.memset(pool_scales[:].bitcast(I32), 0)
        nc.vector.memset(stats[:], 1.0 / COUNT)
        nc.vector.memset(stats[:, 2, 2:3], 0.0)
        nc.vector.memset(key_scales[:].bitcast(I32), 0)
        nc.scalar.activation(flat[:, 0:17:16], flat[:, 1:4:2], ACT.Abs_reciprocal_sqrt, scale=1e8 * COUNT)

        words = k_words[0].rearrange("p t r -> p (t r)").bitcast(I32)
        q_rows = qT[0].rearrange("(p j) w -> p j w", j=PACK)
        nc.sync.dma_start(out=raw_0[:], in_=q_rows[:, :, 0:P])
        nc.sync.dma_start(offsets[:], offs)
        nc.sync.dma_start(out=pool_scales[32:96:4, :].bitcast(I32), in_=k_scales[0].bitcast(I32))
        nc.sync.dma_start(out=pool_words[:].bitcast(I32), in_=words)
        nc.sync.dma_start(out=raw_1[:], in_=q_rows[:, :, P:NQ])

        picked_scales = sb.tile([P, N], U8, name="picked_scales", align_bytes=64)
        nc.vector.tensor_copy(picked_scales[:], pool_scales[:].indirect(offsets[:]))

        def interleave(dst, src):
            nc.scalar.copy(
                out=dst.rearrange("p (g i) j -> p g j i", i=4),
                in_=src.rearrange("p j (g i) -> p g j i", i=4),
            )

        def quantise(c, lo, hi, src):
            nc.vector.quantize_mx(
                out=q_codes[c][:, lo:hi].bitcast(FP8X4),
                scales=q_scales[c][:, lo:hi],
                in_=src.rearrange("p w j -> p (w j)"),
            )

        q_codes = [
            sb.tile([P, P], U32, name="q_codes0", tag="scales_then_codes", align_bytes=64),
            sb.tile([P, P], U32, name="q_codes1", align_bytes=64),
        ]
        q_scales = [sb.tile([P, P], U8, name="q_scales%d" % c, align_bytes=64) for c in range(2)]
        grouped_0 = sb.tile([P, P, PACK], BF16, name="grouped_0", align_bytes=64)
        interleave(grouped_0[:], raw_0[:])
        for r in range(4):
            queue = nc.sync if r % 2 else nc.scalar
            queue.dma_start(out=key_scales[r:P:32, :].bitcast(I32), in_=picked_scales[32 + 4 * r : 96 : 16, :].bitcast(I32))
        quantise(0, 0, P, grouped_0[:])

        keys = [sb.tile([P, HALF], U32, name="keys%d" % h, align_bytes=64) for h in range(2)]
        for lo, hi in ((0, HALF), (HALF, N - LAST), (N - LAST, N)):
            nc.vector.tensor_copy(
                keys[lo // HALF][:, lo % HALF : lo % HALF + hi - lo], pool_words[:].indirect(offsets[:, lo // 16 : hi // 16])
            )
        for lo in (0, PIECE):
            grouped_1 = sb.tile([P, PIECE, PACK], BF16, name="grouped_1_%d" % lo, align_bytes=64)
            interleave(grouped_1[:], raw_1[:, :, lo : lo + PIECE])
            quantise(1, lo, lo + PIECE, grouped_1[:])

        acc = [[ps.tile([P, HALF], F32, name="acc%d%d" % (c, h)) for h in range(2)] for c in range(2)]
        for c, lo, hi in ((0, 0, HALF), (0, HALF, N - LAST), (0, N - LAST, N), (1, 0, HALF), (1, HALF, N)):
            h, cols = lo // HALF, slice(lo % HALF, lo % HALF + hi - lo)
            nc.tensor.matmul_mx(
                out=acc[c][h][:, cols],
                lhsT=q_codes[c][:].bitcast(FP8X4),
                lhsT_scale=q_scales[c][:],
                rhs=keys[h][:, cols].bitcast(FP8X4),
                rhs_scale=key_scales[:, lo:hi],
                start=True,
                stop=True,
            )

        first_squares = sb.tile([P, HALF], BF16, name="first_squares", tag="raw_then_squares")
        later_squares = sb.tile([P, HALF + LINE], F32, name="later_squares")
        squares = {(0, 0): first_squares[:], (0, 1): later_squares[:, 0:HALF], (1, 1): later_squares[:, LINE : HALF + LINE]}
        last = [sb.tile([P, 1], F32, name="ss%d" % c) for c in range(2)]
        ss = {(0, 0): later_squares[:, HALF : HALF + 1], (0, 1): last[0][:], (1, 1): last[1][:]}
        bias = [sb.tile([P, 1], F32, name="bias%d" % c) for c in range(2)]
        rinv = [sb.tile([P, 1], F32, name="rinv%d" % c) for c in range(2)]
        held = sb.tile([P, HALF], F32, name="held")
        terms = sb.tile([P, 3, 2], F32, name="terms")
        res = [sb.tile([P, N], F32, name="res%d" % c) for c in range(2)]

        def square(c, h):
            nc.scalar.activation(squares[c, h], acc[c][h][:], ACT.Square, accum_out=ss[c, h])

        def store(c, lo, hi):
            nc.sync.dma_start(out=out[0, c * P : (c + 1) * P, lo:hi], in_=res[c][:, lo:hi])

        square(0, 0)
        nc.vector.tensor_scalar(bias[0][:], ss[0, 0], eps, None, ALU.add)
        nc.vector.tensor_copy(held[:], acc[0][0][:])
        square(0, 1)
        nc.scalar.activation(rinv[0][:], ss[0, 1], ACT.Abs_reciprocal_sqrt, bias=bias[0][:])
        nc.vector.bn_stats(flat[:, 0:12:2], acc[1][0][:])
        square(1, 1)
        nc.vector.tensor_scalar(res[0][:, 0:HALF], held[:], rinv[0][:], None, ALU.mult)
        store(0, 0, HALF)
        nc.vector.scalar_tensor_tensor(
            terms[:], stats[:, :, 2:6:2], float(COUNT), stats[:, :, 2:4], ALU.mult, ALU.mult, accum_out=bias[1][:]
        )
        nc.vector.tensor_scalar(res[0][:, HALF:N], acc[0][1][:], rinv[0][:], None, ALU.mult)
        store(0, HALF, N)
        nc.scalar.activation(rinv[1][:], ss[1, 1], ACT.Abs_reciprocal_sqrt, bias=bias[1][:])
        nc.vector.tensor_scalar(res[1][:, 0:HALF], acc[1][0][:], rinv[1][:], None, ALU.mult)
        nc.scalar.activation(res[1][:, HALF:N], acc[1][1][:], ACT.Copy, scale=rinv[1][:])
        store(1, 0, N)
